import numpy as np
import ml_dtypes


def mxq(x, axis, fmt="e4m3"):
    dtype, down = {"e4m3": (ml_dtypes.float8_e4m3fn, 7), "e5m2": (ml_dtypes.float8_e5m2, 14)}[fmt]
    v = np.moveaxis(np.asarray(x, np.float32).astype(ml_dtypes.bfloat16).astype(np.float64), axis, -1)
    blocks = v.reshape(v.shape[:-1] + (-1, 32))
    amax = np.abs(blocks).max(-1, keepdims=True)
    byte = np.maximum(np.where(amax > 0, np.frexp(amax)[1] - 1 + 127, 0) - down, 1)
    scale = np.exp2(byte - 127.0)
    codes = (blocks / scale).astype(np.float32).astype(dtype).astype(np.float64)
    return np.moveaxis((codes * scale).reshape(v.shape), -1, axis)


WIDE = False


def mx_kscale(k):
    if not WIDE:
        return np.ones(k)
    levels = np.array([10, -10, 5, -5, 0])
    if k % 512:
        return np.exp2(np.random.permutation(np.resize(levels, k // 32))).repeat(32)
    a = np.empty((k // 512, 16))
    for p in range(k // 512):
        a[p, :8] = np.random.permutation(np.resize(levels, 8))
        for g in range(8):
            far = levels[np.abs(levels - a[p, g]) >= 10]
            a[p, g + 8] = far[np.random.randint(len(far))]
    return np.exp2(a.ravel()).repeat(32)


def f64(x):
    return np.asarray(x).astype(np.float64)


def striped(idx):
    return np.tile(np.asarray(idx).reshape(-1, 16).T, (8, 1)).astype(np.uint16)


def unstriped(offs):
    return offs[:16].T.reshape(-1).astype(np.int64)


E2M1 = np.array([0.0, 0.5, 1.0, 1.5, 2.0, 3.0, 4.0, 6.0, -0.0, -0.5, -1.0, -1.5, -2.0, -3.0, -4.0, -6.0])


def pack_weight(w, fmt):
    k, n = w.shape
    w = f64(np.asarray(w, np.float32).astype(ml_dtypes.bfloat16)).reshape(k // 32, 32, n)
    amax = np.abs(w).max(1)
    if fmt == "e4m3":
        byte = np.frexp(amax)[1] - 1 + 127 - 7
    else:
        mant, ex = np.frexp(amax / 6.0)
        byte = np.where(mant > 0.5, ex, ex - 1) + 127
    byte = np.clip(np.where(amax > 0, byte, 1), 1, 254)
    scaled = (w * np.exp2(127.0 - byte)[:, None, :]).reshape(k, n).astype(np.float32)
    by_word = np.ascontiguousarray(scaled.reshape(k // 512, 128, 4, n).transpose(0, 1, 3, 2))
    if fmt == "e4m3":
        words = by_word.astype(ml_dtypes.float8_e4m3fn).view(np.uint8)
    else:
        c = by_word.astype(ml_dtypes.float4_e2m1fn).view(np.uint8) & 0xF
        words = (c[..., 0::2] | (c[..., 1::2] << 4)).reshape(k // 512, 128, 2 * n)
    return np.ascontiguousarray(words), np.ascontiguousarray(byte.astype(np.uint8).reshape(k // 512, 16, n))


def unpack_weight(words, scales, fmt):
    g, _, n = scales.shape
    words = np.ascontiguousarray(words).reshape(g, 128, n, -1)
    if fmt == "e4m3":
        vals = words.view(ml_dtypes.float8_e4m3fn).astype(np.float64)
    else:
        nib = np.empty((g, 128, n, 4), np.uint8)
        nib[..., 0::2] = words & 0xF
        nib[..., 1::2] = words >> 4
        vals = E2M1[nib]
    vals = vals * np.repeat(np.exp2(scales.astype(np.float64) - 127.0), 8, axis=1)[..., None]
    return vals.transpose(0, 1, 3, 2).reshape(g * 512, n)


D, E, T, I, Q = 512, 512, 2048, 512, 128


def setup_inputs():
    n = np.random.standard_normal
    idx = np.random.permutation(T)[:I]
    fd = mx_kscale(D)
    fe = mx_kscale(E)
    keysp = pack_weight(n((D, T)) / fd[:, None], "e4m3")
    valsp = pack_weight(n((E, T)) / fe[:, None], "e4m3")
    return {
        "query": (n((D, Q)) * 1.0 / np.sqrt(D) * fd[:, None]).astype(np.float32),
        "keys_words": keysp[0],
        "keys_scales": keysp[1],
        "aim": (np.random.uniform(0.5, 2.0, (Q, 1))).astype(np.float32),
        "soft": (np.random.uniform(0.5, 2.0, (Q, 1))).astype(np.float32),
        "gout": (n((E, Q)) * 1 / np.sqrt(E) * fe[:, None]).astype(np.float32),
        "vals_words": valsp[0],
        "vals_scales": valsp[1],
        "base": (0.5 * n((Q, I))).astype(np.float32),
        "offs": striped(idx),
    }


def reference(query, keys_words, keys_scales, aim, soft, gout, vals_words, vals_scales, base, offs):
    idx = unstriped(offs)
    keysu = unpack_weight(keys_words, keys_scales, "e4m3")
    valsu = unpack_weight(vals_words, vals_scales, "e4m3")
    queryq = mxq(f64(query), 0, "e4m3")
    keysidxg = keysu[:, idx]
    a = queryq.T @ keysidxg
    p = 1.0 / (np.square(f64(aim) - a) + f64(soft))
    z = np.sum(p, axis=1, keepdims=True)
    goutq = mxq(f64(gout), 0, "e4m3")
    valsidxg = valsu[:, idx]
    c0 = goutq.T @ valsidxg
    dz = np.sum(c0 * p / np.square(z) * (-1.0), axis=1, keepdims=True)
    dp = c0 / z + dz
    da = dp * (-1.0) / np.square(np.square(f64(aim) - a) + f64(soft)) * (f64(aim) - a) * 2.0 * (-1.0)
    hda = da * 512.0 * 2.0 * 512.0
    hdp = hda * (-1.0) * 2.0 * (f64(aim) - a) / np.square(np.square(f64(aim) - a) + f64(soft)) * (-1.0)
    hdz = np.sum(hdp, axis=1, keepdims=True)
    hz = np.sum(hdp * c0 / np.square(z) * (-1.0), axis=1, keepdims=True) + np.sum(hdz * (-1.0) * c0 * p / np.square(np.square(z)) * (-1.0), axis=1, keepdims=True) * z * 2.0
    hp = hdz * (-1.0) / np.square(z) * c0 + hz
    ha = hda * (-1.0) * 2.0 * (f64(aim) - a) * dp * (-1.0) / np.square(np.square(np.square(f64(aim) - a) + f64(soft))) * (-1.0) * (np.square(f64(aim) - a) + f64(soft)) * 2.0 * (f64(aim) - a) * 2.0 * (-1.0) - hda * (-1.0) * 2.0 * dp * (-1.0) / np.square(np.square(f64(aim) - a) + f64(soft)) - hp * (-1.0) / np.square(np.square(f64(aim) - a) + f64(soft)) * (f64(aim) - a) * 2.0
    y = ha + f64(base)
    return y

@@ -1,0 +1,150 @@
+from contextlib import ExitStack
+
+import concourse.mybir as mybir
+
+D, E, T, I, Q = 512, 512, 2048, 512, 128
+FLOPS = 2 * 2 * 512 * Q * I
+
+F32 = mybir.dt.float32
+BF16 = mybir.dt.bfloat16
+I32 = mybir.dt.int32
+U32 = mybir.dt.uint32
+U16 = mybir.dt.uint16
+U8 = mybir.dt.uint8
+FP8X4 = mybir.dt.float8_e4m3fn_x4
+ACT = mybir.ActivationFunctionType
+ALU = mybir.AluOpType
+
+P = 128
+PACK = 4
+HALF = I // 2
+VAL_ROW = 4
+PENALTY = 4.0 * 512.0 * 2.0 * 512.0
+
+
+def tile_attend_gpnearpoint_kernel(tc, query, keys_words, keys_scales, aim, soft, gout, vals_words, vals_scales, base, offs, out):
+    nc = tc.nc
+    with ExitStack() as ctx:
+        held = ctx.enter_context(tc.tile_pool(name="held", bufs=1))
+        psum = ctx.enter_context(tc.psum_pool(name="psum", bufs=1))
+
+        def wide(name):
+            return held.tile([P, I], F32, name=name, align_bytes=64)
+
+        def column(name):
+            return held.tile([P, 1], F32, name=name)
+
+        halves = [slice(h * HALF, (h + 1) * HALF) for h in range(2)]
+
+        offsets = held.tile([P, I // 16], U16, name="offsets")
+        nc.sync.dma_start(offsets[:], offs)
+
+        key_scale_pool = held.tile([P, T], U8, name="key_scale_pool", align_bytes=64)
+        val_scale_pool = held.tile([P, T], U8, name="val_scale_pool", align_bytes=64)
+        nc.vector.memset(key_scale_pool[:].bitcast(I32), 0)
+        nc.vector.memset(val_scale_pool[:].bitcast(I32), 0)
+
+        one = column("one")
+        warm = column("warm")
+        nc.gpsimd.memset(one[:], 1.0)
+        nc.scalar.activation(warm[:], one[:], ACT.Ln)
+
+        aim_col = column("aim_col")
+        soft_col = column("soft_col")
+        nc.gpsimd.dma_start(aim_col[:], aim)
+        nc.gpsimd.dma_start(soft_col[:], soft)
+
+        def load_rows(name, src):
+            raw = held.tile([P, PACK, Q], F32, name=name)
+            nc.sync.dma_start(raw[:], src.rearrange("(p j) w -> p j w", j=PACK))
+            return raw
+
+        def load_scales(pool_tile, src, first_row):
+            for r in range(4):
+                nc.sync.dma_start(pool_tile[first_row + r : P : 32, :].bitcast(I32), src[0, r:16:4, :].bitcast(I32))
+
+        def load_words(name, src):
+            words = held.tile([P, T], U32, name=name, align_bytes=64)
+            nc.sync.dma_start(words[:].bitcast(I32), src[0].rearrange("p n t -> p (n t)").bitcast(I32))
+            return words
+
+        query_raw = load_rows("query_raw", query)
+        load_scales(key_scale_pool, keys_scales, 0)
+        key_word_pool = load_words("key_word_pool", keys_words)
+        gout_raw = load_rows("gout_raw", gout)
+        load_scales(val_scale_pool, vals_scales, VAL_ROW)
+        val_word_pool = load_words("val_word_pool", vals_words)
+        base_sb = wide("base_sb")
+        nc.sync.dma_start(base_sb[:], base)
+
+        def quantize(name, raw, cast):
+            grouped = held.tile([P, Q, PACK], BF16, name=name + "_grouped", align_bytes=64)
+            codes = held.tile([P, Q], U32, name=name + "_codes", align_bytes=64)
+            scales = held.tile([P, Q], U8, name=name + "_scales", align_bytes=64)
+            cast(grouped[:], raw[:].rearrange("p j w -> p w j"))
+            nc.vector.quantize_mx(out=codes[:].bitcast(FP8X4), scales=scales[:], in_=grouped[:].rearrange("p w j -> p (w j)"))
+            return codes, scales
+
+        def gather_scales(name, pool_tile):
+            picked = held.tile([P, I], U8, name=name, align_bytes=64)
+            nc.vector.tensor_copy(picked[:], pool_tile[:].indirect(offsets[:]))
+            return picked
+
+        def gather_and_multiply(name, pool_tile, picked_scales, first_row, codes, scales, outs):
+            for h in range(2):
+                picked = held.tile([P, HALF], U32, name=name + str(h), align_bytes=64)
+                nc.vector.tensor_copy(picked[:], pool_tile[:].indirect(offsets[:, h * HALF // 16 : (h + 1) * HALF // 16]))
+                nc.tensor.matmul_mx(out=outs[h], lhsT=codes[:].bitcast(FP8X4), lhsT_scale=scales[:],
+                                    rhs=picked[:].bitcast(FP8X4), rhs_scale=picked_scales[first_row:P, halves[h]],
+                                    start=True, stop=True)
+
+        query_codes, query_scales = quantize("query", query_raw, nc.scalar.copy)
+        key_scales = gather_scales("key_scales", key_scale_pool)
+        score = [psum.tile([P, I], F32, name="score" + str(h)) for h in range(2)]
+        score = [s[:, 0:HALF] for s in score]
+        gather_and_multiply("key_words", key_word_pool, key_scales, 0, query_codes, query_scales, score)
+
+        usq, root, part, part2, slope = wide("usq"), wide("root"), wide("part"), wide("part2"), wide("slope")
+        for h in range(2):
+            c = halves[h]
+            nc.scalar.activation(usq[:, c], score[h], ACT.Square, bias=aim_col[:], scale=-1.0)
+            nc.scalar.activation(root[:, c], usq[:, c], ACT.Ln, bias=soft_col[:])
+        z = column("z")
+        nc.scalar.activation(part[:], root[:], ACT.Exp, scale=-1.0, accum_out=z[:])
+        curve = wide("curve")
+        for h in range(2):
+            c = halves[h]
+            nc.scalar.activation(part2[:, c], root[:, c], ACT.Exp, scale=-2.0)
+            nc.scalar.activation(slope[:, c], part[:, c], ACT.Identity, bias=-0.75, scale=soft_col[:])
+            nc.gpsimd.tensor_tensor(curve[:, c], slope[:, c], part2[:, c], ALU.mult)
+
+        gout_codes, gout_scales = quantize("gout", gout_raw, nc.vector.tensor_copy)
+        val_scales = gather_scales("val_scales", val_scale_pool)
+        cbank = psum.tile([P, I], F32, name="cbank")
+        gather_and_multiply("val_words", val_word_pool, val_scales, VAL_ROW, gout_codes, gout_scales,
+                            [cbank[:, halves[0]], cbank[:, halves[1]]])
+
+        rz, rz_half, alpha, beta = column("rz"), column("rz_half"), column("alpha"), column("beta")
+        nc.vector.reciprocal(rz[:], z[:])
+        nc.gpsimd.tensor_scalar(rz_half[:], rz[:], 0.5, 0.0, ALU.mult, ALU.add)
+        nc.gpsimd.tensor_scalar(alpha[:], rz[:], rz[:], 4.0 * PENALTY, ALU.mult, ALU.mult)
+        nc.gpsimd.tensor_tensor(beta[:], alpha[:], rz_half[:], ALU.mult)
+
+        g, scratch, t, v, y1, y2, y, tsq = [wide(n) for n in ("g", "scratch", "t", "v", "y1", "y2", "y", "tsq")]
+        mean, a1, bsum, b1 = column("mean"), column("a1"), column("bsum"), column("b1")
+        nc.vector.scalar_tensor_tensor(scratch[:], cbank[:], rz[:], part[:], ALU.mult, ALU.mult, accum_out=mean[:])
+        for h in range(2):
+            nc.vector.scalar_tensor_tensor(g[:, halves[h]], score[h], aim_col[:], part2[:, halves[h]], ALU.subtract, ALU.mult)
+        nc.vector.scalar_tensor_tensor(t[:], cbank[:], mean[:], g[:], ALU.subtract, ALU.mult)
+        nc.vector.scalar_tensor_tensor(v[:], cbank[:], mean[:], curve[:], ALU.subtract, ALU.mult)
+        nc.scalar.activation(tsq[:], t[:], ACT.Square, accum_out=bsum[:])
+        nc.scalar.activation(b1[:], bsum[:], ACT.Copy, scale=beta[:])
+        nc.vector.scalar_tensor_tensor(scratch[:], t[:], rz_half[:], g[:], ALU.mult, ALU.mult, accum_out=a1[:])
+        nc.vector.scalar_tensor_tensor(y2[:], g[:], b1[:], base_sb[:], ALU.mult, ALU.add)
+        for h in range(2):
+            c = halves[h]
+            nc.vector.scalar_tensor_tensor(y1[:, c], v[:, c], a1[:], t[:, c], ALU.add, ALU.mult)
+        for h in range(2):
+            c = halves[h]
+            nc.vector.scalar_tensor_tensor(y[:, c], y1[:, c], alpha[:], y2[:, c], ALU.mult, ALU.add)
+            (nc.sync if h == 0 else nc.scalar).dma_start(out[:, c], y[:, c])

@@ -41,18 +41,17 @@ def tile_attend_gpnearpoint_kernel(tc, query, keys_words, keys_scales, aim, soft
 
         key_scale_pool = held.tile([P, T], U8, name="key_scale_pool", align_bytes=64)
         val_scale_pool = held.tile([P, T], U8, name="val_scale_pool", align_bytes=64)
-        nc.vector.memset(key_scale_pool[:].bitcast(I32), 0)
-        nc.vector.memset(val_scale_pool[:].bitcast(I32), 0)
+        nc.gpsimd.memset(key_scale_pool[:].bitcast(I32), 0)
 
         one = column("one")
         warm = column("warm")
-        nc.gpsimd.memset(one[:], 1.0)
+        nc.vector.memset(one[:], 1.0)
+        nc.vector.memset(val_scale_pool[:].bitcast(I32), 0)
         nc.scalar.activation(warm[:], one[:], ACT.Ln)
 
         aim_col = column("aim_col")
         soft_col = column("soft_col")
         nc.gpsimd.dma_start(aim_col[:], aim)
-        nc.gpsimd.dma_start(soft_col[:], soft)
 
         def load_rows(name, src):
             raw = held.tile([P, PACK, Q], F32, name=name)
@@ -64,13 +63,16 @@ def tile_attend_gpnearpoint_kernel(tc, query, keys_words, keys_scales, aim, soft
                 nc.sync.dma_start(pool_tile[first_row + r : P : 32, :].bitcast(I32), src[0, r:16:4, :].bitcast(I32))
 
         def load_words(name, src):
-            words = held.tile([P, T], U32, name=name, align_bytes=64)
+            words = held.tile([P, T], U32, name=name, tag=name, align_bytes=64)
             nc.sync.dma_start(words[:].bitcast(I32), src[0].rearrange("p n t -> p (n t)").bitcast(I32))
             return words
 
         query_raw = load_rows("query_raw", query)
         load_scales(key_scale_pool, keys_scales, 0)
         key_word_pool = load_words("key_word_pool", keys_words)
+        nc.sync.dma_start(soft_col[:], soft)
+        soft2 = column("soft2")
+        nc.gpsimd.tensor_scalar(soft2[:], soft_col[:], 2.0, 0.0, ALU.mult, ALU.add)
         gout_raw = load_rows("gout_raw", gout)
         load_scales(val_scale_pool, vals_scales, VAL_ROW)
         val_word_pool = load_words("val_word_pool", vals_words)
@@ -91,56 +93,64 @@ def tile_attend_gpnearpoint_kernel(tc, query, keys_words, keys_scales, aim, soft
             return picked
 
         def gather_and_multiply(name, pool_tile, picked_scales, first_row, codes, scales, outs):
+            picked = held.tile([P, I], U32, name=name, align_bytes=64)
             for h in range(2):
-                picked = held.tile([P, HALF], U32, name=name + str(h), align_bytes=64)
-                nc.vector.tensor_copy(picked[:], pool_tile[:].indirect(offsets[:, h * HALF // 16 : (h + 1) * HALF // 16]))
-                nc.tensor.matmul_mx(out=outs[h], lhsT=codes[:].bitcast(FP8X4), lhsT_scale=scales[:],
-                                    rhs=picked[:].bitcast(FP8X4), rhs_scale=picked_scales[first_row:P, halves[h]],
+                nc.vector.tensor_copy(picked[:, halves[h]], pool_tile[:].indirect(offsets[:, h * HALF // 16 : (h + 1) * HALF // 16]))
+            for c, target in outs:
+                nc.tensor.matmul_mx(out=target, lhsT=codes[:].bitcast(FP8X4), lhsT_scale=scales[:],
+                                    rhs=picked[:, c].bitcast(FP8X4), rhs_scale=picked_scales[first_row:P, c],
                                     start=True, stop=True)
 
         query_codes, query_scales = quantize("query", query_raw, nc.scalar.copy)
         key_scales = gather_scales("key_scales", key_scale_pool)
-        score = [psum.tile([P, I], F32, name="score" + str(h)) for h in range(2)]
-        score = [s[:, 0:HALF] for s in score]
+        pieces = [slice(0, 256), slice(256, 384), slice(384, 512)]
+        banks = [psum.tile([P, I], F32, name="score" + str(h)) for h in range(3)]
+        score = [(c, b[:, 0 : c.stop - c.start]) for c, b in zip(pieces, banks)]
         gather_and_multiply("key_words", key_word_pool, key_scales, 0, query_codes, query_scales, score)
 
         usq, root, part, part2, slope = wide("usq"), wide("root"), wide("part"), wide("part2"), wide("slope")
-        for h in range(2):
-            c = halves[h]
-            nc.scalar.activation(usq[:, c], score[h], ACT.Square, bias=aim_col[:], scale=-1.0)
-            nc.scalar.activation(root[:, c], usq[:, c], ACT.Ln, bias=soft_col[:])
+        for group in (score[:1], score[1:]):
+            for c, s in group:
+                nc.scalar.activation(usq[:, c], s, ACT.Square, bias=aim_col[:], scale=-1.0)
+            for c, s in group:
+                nc.scalar.activation(root[:, c], usq[:, c], ACT.Ln, bias=soft_col[:])
         z = column("z")
         nc.scalar.activation(part[:], root[:], ACT.Exp, scale=-1.0, accum_out=z[:])
         curve = wide("curve")
         for h in range(2):
             c = halves[h]
             nc.scalar.activation(part2[:, c], root[:, c], ACT.Exp, scale=-2.0)
-            nc.scalar.activation(slope[:, c], part[:, c], ACT.Identity, bias=-0.75, scale=soft_col[:])
+            nc.scalar.activation(slope[:, c], part[:, c], ACT.Identity, bias=-1.5, scale=soft2[:])
             nc.gpsimd.tensor_tensor(curve[:, c], slope[:, c], part2[:, c], ALU.mult)
 
         gout_codes, gout_scales = quantize("gout", gout_raw, nc.vector.tensor_copy)
         val_scales = gather_scales("val_scales", val_scale_pool)
         cbank = psum.tile([P, I], F32, name="cbank")
         gather_and_multiply("val_words", val_word_pool, val_scales, VAL_ROW, gout_codes, gout_scales,
-                            [cbank[:, halves[0]], cbank[:, halves[1]]])
+                            [(c, cbank[:, c]) for c in halves])
 
-        rz, rz_half, alpha, beta = column("rz"), column("rz_half"), column("alpha"), column("beta")
-        nc.vector.reciprocal(rz[:], z[:])
-        nc.gpsimd.tensor_scalar(rz_half[:], rz[:], 0.5, 0.0, ALU.mult, ALU.add)
-        nc.gpsimd.tensor_scalar(alpha[:], rz[:], rz[:], 4.0 * PENALTY, ALU.mult, ALU.mult)
-        nc.gpsimd.tensor_tensor(beta[:], alpha[:], rz_half[:], ALU.mult)
+        reused = held.tile([P, I + 8], F32, name="reused", tag="val_word_pool", align_bytes=64)
+        g, rz = reused[:, 0:I], reused[:, I : I + 1]
+        alpha, beta = column("alpha"), column("beta")
+        nc.vector.reciprocal(rz, z[:])
+        nc.scalar.activation(alpha[:], rz, ACT.Square, scale=2048.0)
+        nc.scalar.activation(beta[:], alpha[:], ACT.Copy, scale=rz)
 
-        g, scratch, t, v, y1, y2, y, tsq = [wide(n) for n in ("g", "scratch", "t", "v", "y1", "y2", "y", "tsq")]
+        scratch, t, v, y1, y2, y, tsq = [wide(n) for n in ("scratch", "t", "v", "y1", "y2", "y", "tsq")]
         mean, a1, bsum, b1 = column("mean"), column("a1"), column("bsum"), column("b1")
-        nc.vector.scalar_tensor_tensor(scratch[:], cbank[:], rz[:], part[:], ALU.mult, ALU.mult, accum_out=mean[:])
-        for h in range(2):
-            nc.vector.scalar_tensor_tensor(g[:, halves[h]], score[h], aim_col[:], part2[:, halves[h]], ALU.subtract, ALU.mult)
-        nc.vector.scalar_tensor_tensor(t[:], cbank[:], mean[:], g[:], ALU.subtract, ALU.mult)
-        nc.vector.scalar_tensor_tensor(v[:], cbank[:], mean[:], curve[:], ALU.subtract, ALU.mult)
+        msum = column("msum")
+        nc.vector.scalar_tensor_tensor(scratch[:], cbank[:], 1.0, part[:], ALU.mult, ALU.mult, accum_out=msum[:])
+        for h, (c, s) in enumerate(score):
+            nc.vector.scalar_tensor_tensor(g[:, c], s, aim_col[:], part2[:, c], ALU.subtract, ALU.mult)
+            if h == 0:
+                nc.vector.tensor_tensor(mean[:], msum[:], rz, ALU.mult)
+        nc.vector.scalar_tensor_tensor(t[:], cbank[:], mean[:], g, ALU.subtract, ALU.mult)
+        for c in halves:
+            nc.vector.scalar_tensor_tensor(v[:, c], cbank[:, c], mean[:], curve[:, c], ALU.subtract, ALU.mult)
         nc.scalar.activation(tsq[:], t[:], ACT.Square, accum_out=bsum[:])
         nc.scalar.activation(b1[:], bsum[:], ACT.Copy, scale=beta[:])
-        nc.vector.scalar_tensor_tensor(scratch[:], t[:], rz_half[:], g[:], ALU.mult, ALU.mult, accum_out=a1[:])
-        nc.vector.scalar_tensor_tensor(y2[:], g[:], b1[:], base_sb[:], ALU.mult, ALU.add)
+        nc.vector.scalar_tensor_tensor(scratch[:], t[:], rz, g, ALU.mult, ALU.mult, accum_out=a1[:])
+        nc.vector.scalar_tensor_tensor(y2[:], g, b1[:], base_sb[:], ALU.mult, ALU.add)
         for h in range(2):
             c = halves[h]
             nc.vector.scalar_tensor_tensor(y1[:, c], v[:, c], a1[:], t[:, c], ALU.add, ALU.mult)

from contextlib import ExitStack

import concourse.mybir as mybir

D, E, T, I, Q = 512, 512, 2048, 512, 128
FLOPS = 2 * 2 * 512 * Q * I

F32 = mybir.dt.float32
BF16 = mybir.dt.bfloat16
I32 = mybir.dt.int32
U32 = mybir.dt.uint32
U16 = mybir.dt.uint16
U8 = mybir.dt.uint8
FP8X4 = mybir.dt.float8_e4m3fn_x4
ACT = mybir.ActivationFunctionType
ALU = mybir.AluOpType

P = 128
PACK = 4
HALF = I // 2
VAL_ROW = 4
PENALTY = 4.0 * 512.0 * 2.0 * 512.0


def tile_attend_gpnearpoint_kernel(tc, query, keys_words, keys_scales, aim, soft, gout, vals_words, vals_scales, base, offs, out):
    nc = tc.nc
    with ExitStack() as ctx:
        held = ctx.enter_context(tc.tile_pool(name="held", bufs=1))
        psum = ctx.enter_context(tc.psum_pool(name="psum", bufs=1))

        def wide(name):
            return held.tile([P, I], F32, name=name, align_bytes=64)

        def column(name):
            return held.tile([P, 1], F32, name=name)

        halves = [slice(h * HALF, (h + 1) * HALF) for h in range(2)]

        offsets = held.tile([P, I // 16], U16, name="offsets")
        nc.sync.dma_start(offsets[:], offs)

        key_scale_pool = held.tile([P, T], U8, name="key_scale_pool", align_bytes=64)
        val_scale_pool = held.tile([P, T], U8, name="val_scale_pool", align_bytes=64)
        nc.gpsimd.memset(key_scale_pool[:].bitcast(I32), 0)

        one = column("one")
        warm = column("warm")
        nc.vector.memset(one[:], 1.0)
        nc.vector.memset(val_scale_pool[:].bitcast(I32), 0)
        nc.scalar.activation(warm[:], one[:], ACT.Ln)

        aim_col = column("aim_col")
        soft_col = column("soft_col")
        nc.gpsimd.dma_start(aim_col[:], aim)

        def load_rows(name, src):
            raw = held.tile([P, PACK, Q], F32, name=name)
            nc.sync.dma_start(raw[:], src.rearrange("(p j) w -> p j w", j=PACK))
            return raw

        def load_scales(pool_tile, src, first_row):
            for r in range(4):
                nc.sync.dma_start(pool_tile[first_row + r : P : 32, :].bitcast(I32), src[0, r:16:4, :].bitcast(I32))

        def load_words(name, src):
            words = held.tile([P, T], U32, name=name, tag=name, align_bytes=64)
            nc.sync.dma_start(words[:].bitcast(I32), src[0].rearrange("p n t -> p (n t)").bitcast(I32))
            return words

        query_raw = load_rows("query_raw", query)
        load_scales(key_scale_pool, keys_scales, 0)
        key_word_pool = load_words("key_word_pool", keys_words)
        nc.sync.dma_start(soft_col[:], soft)
        soft2 = column("soft2")
        nc.gpsimd.tensor_scalar(soft2[:], soft_col[:], 2.0, 0.0, ALU.mult, ALU.add)
        gout_raw = load_rows("gout_raw", gout)
        load_scales(val_scale_pool, vals_scales, VAL_ROW)
        val_word_pool = load_words("val_word_pool", vals_words)
        base_sb = wide("base_sb")
        nc.sync.dma_start(base_sb[:], base)

        def quantize(name, raw, cast):
            grouped = held.tile([P, Q, PACK], BF16, name=name + "_grouped", align_bytes=64)
            codes = held.tile([P, Q], U32, name=name + "_codes", align_bytes=64)
            scales = held.tile([P, Q], U8, name=name + "_scales", align_bytes=64)
            cast(grouped[:], raw[:].rearrange("p j w -> p w j"))
            nc.vector.quantize_mx(out=codes[:].bitcast(FP8X4), scales=scales[:], in_=grouped[:].rearrange("p w j -> p (w j)"))
            return codes, scales

        def gather_scales(name, pool_tile):
            picked = held.tile([P, I], U8, name=name, align_bytes=64)
            nc.vector.tensor_copy(picked[:], pool_tile[:].indirect(offsets[:]))
            return picked

        def gather_and_multiply(name, pool_tile, picked_scales, first_row, codes, scales, outs):
            picked = held.tile([P, I], U32, name=name, align_bytes=64)
            for h in range(2):
                nc.vector.tensor_copy(picked[:, halves[h]], pool_tile[:].indirect(offsets[:, h * HALF // 16 : (h + 1) * HALF // 16]))
            for c, target in outs:
                nc.tensor.matmul_mx(out=target, lhsT=codes[:].bitcast(FP8X4), lhsT_scale=scales[:],
                                    rhs=picked[:, c].bitcast(FP8X4), rhs_scale=picked_scales[first_row:P, c],
                                    start=True, stop=True)

        query_codes, query_scales = quantize("query", query_raw, nc.scalar.copy)
        key_scales = gather_scales("key_scales", key_scale_pool)
        pieces = [slice(0, 256), slice(256, 384), slice(384, 512)]
        banks = [psum.tile([P, I], F32, name="score" + str(h)) for h in range(3)]
        score = [(c, b[:, 0 : c.stop - c.start]) for c, b in zip(pieces, banks)]
        gather_and_multiply("key_words", key_word_pool, key_scales, 0, query_codes, query_scales, score)

        usq, root, part, part2, slope = wide("usq"), wide("root"), wide("part"), wide("part2"), wide("slope")
        for group in (score[:1], score[1:]):
            for c, s in group:
                nc.scalar.activation(usq[:, c], s, ACT.Square, bias=aim_col[:], scale=-1.0)
            for c, s in group:
                nc.scalar.activation(root[:, c], usq[:, c], ACT.Ln, bias=soft_col[:])
        z = column("z")
        nc.scalar.activation(part[:], root[:], ACT.Exp, scale=-1.0, accum_out=z[:])
        curve = wide("curve")
        for h in range(2):
            c = halves[h]
            nc.scalar.activation(part2[:, c], root[:, c], ACT.Exp, scale=-2.0)
            nc.scalar.activation(slope[:, c], part[:, c], ACT.Identity, bias=-1.5, scale=soft2[:])
            nc.gpsimd.tensor_tensor(curve[:, c], slope[:, c], part2[:, c], ALU.mult)

        gout_codes, gout_scales = quantize("gout", gout_raw, nc.vector.tensor_copy)
        val_scales = gather_scales("val_scales", val_scale_pool)
        cbank = psum.tile([P, I], F32, name="cbank")
        gather_and_multiply("val_words", val_word_pool, val_scales, VAL_ROW, gout_codes, gout_scales,
                            [(c, cbank[:, c]) for c in halves])

        reused = held.tile([P, I + 8], F32, name="reused", tag="val_word_pool", align_bytes=64)
        g, rz = reused[:, 0:I], reused[:, I : I + 1]
        alpha, beta = column("alpha"), column("beta")
        nc.vector.reciprocal(rz, z[:])
        nc.scalar.activation(alpha[:], rz, ACT.Square, scale=2048.0)
        nc.scalar.activation(beta[:], alpha[:], ACT.Copy, scale=rz)

        scratch, t, v, y1, y2, y, tsq = [wide(n) for n in ("scratch", "t", "v", "y1", "y2", "y", "tsq")]
        mean, a1, bsum, b1 = column("mean"), column("a1"), column("bsum"), column("b1")
        msum = column("msum")
        nc.vector.scalar_tensor_tensor(scratch[:], cbank[:], 1.0, part[:], ALU.mult, ALU.mult, accum_out=msum[:])
        for h, (c, s) in enumerate(score):
            nc.vector.scalar_tensor_tensor(g[:, c], s, aim_col[:], part2[:, c], ALU.subtract, ALU.mult)
            if h == 0:
                nc.vector.tensor_tensor(mean[:], msum[:], rz, ALU.mult)
        nc.vector.scalar_tensor_tensor(t[:], cbank[:], mean[:], g, ALU.subtract, ALU.mult)
        for c in halves:
            nc.vector.scalar_tensor_tensor(v[:, c], cbank[:, c], mean[:], curve[:, c], ALU.subtract, ALU.mult)
        nc.scalar.activation(tsq[:], t[:], ACT.Square, accum_out=bsum[:])
        nc.scalar.activation(b1[:], bsum[:], ACT.Copy, scale=beta[:])
        nc.vector.scalar_tensor_tensor(scratch[:], t[:], rz, g, ALU.mult, ALU.mult, accum_out=a1[:])
        nc.vector.scalar_tensor_tensor(y2[:], g, b1[:], base_sb[:], ALU.mult, ALU.add)
        for h in range(2):
            c = halves[h]
            nc.vector.scalar_tensor_tensor(y1[:, c], v[:, c], a1[:], t[:, c], ALU.add, ALU.mult)
        for h in range(2):
            c = halves[h]
            nc.vector.scalar_tensor_tensor(y[:, c], y1[:, c], alpha[:], y2[:, c], ALU.mult, ALU.add)
            (nc.sync if h == 0 else nc.scalar).dma_start(out[:, c], y[:, c])
